import numpy as np
import ml_dtypes


def mxq(x, axis, fmt="e4m3"):
    dtype, down = {"e4m3": (ml_dtypes.float8_e4m3fn, 7), "e5m2": (ml_dtypes.float8_e5m2, 14)}[fmt]
    v = np.moveaxis(np.asarray(x, np.float32).astype(ml_dtypes.bfloat16).astype(np.float64), axis, -1)
    blocks = v.reshape(v.shape[:-1] + (-1, 32))
    amax = np.abs(blocks).max(-1, keepdims=True)
    byte = np.maximum(np.where(amax > 0, np.frexp(amax)[1] - 1 + 127, 0) - down, 1)
    scale = np.exp2(byte - 127.0)
    codes = (blocks / scale).astype(np.float32).astype(dtype).astype(np.float64)
    return np.moveaxis((codes * scale).reshape(v.shape), -1, axis)


WIDE = False


def mx_kscale(k):
    if not WIDE:
        return np.ones(k)
    levels = np.array([10, -10, 5, -5, 0])
    if k % 512:
        return np.exp2(np.random.permutation(np.resize(levels, k // 32))).repeat(32)
    a = np.empty((k // 512, 16))
    for p in range(k // 512):
        a[p, :8] = np.random.permutation(np.resize(levels, 8))
        for g in range(8):
            far = levels[np.abs(levels - a[p, g]) >= 10]
            a[p, g + 8] = far[np.random.randint(len(far))]
    return np.exp2(a.ravel()).repeat(32)


def f64(x):
    return np.asarray(x).astype(np.float64)


def striped(idx):
    return np.tile(idx.reshape(-1, 16).T, (8, 1)).astype(np.uint16)


def unstriped(offs):
    return offs[:16].T.reshape(-1).astype(np.int64)


def pack_weight(w):
    k, n = w.shape
    w = f64(np.asarray(w, np.float32).astype(ml_dtypes.bfloat16)).reshape(k // 32, 32, n)
    amax = np.abs(w).max(1)
    byte = np.clip(np.where(amax > 0, np.frexp(amax)[1] - 1 + 127 - 7, 1), 1, 254)
    scaled = (w * np.exp2(127.0 - byte)[:, None, :]).reshape(k, n).astype(np.float32)
    words = np.ascontiguousarray(scaled.reshape(k // 512, 128, 4, n).transpose(0, 1, 3, 2)).astype(ml_dtypes.float8_e4m3fn).view(np.uint8)
    return words, np.ascontiguousarray(byte.astype(np.uint8).reshape(k // 512, 16, n))


def unpack_weight(words, scales):
    g, p, n, _ = words.shape
    vals = np.ascontiguousarray(words).view(ml_dtypes.float8_e4m3fn).astype(np.float64) * np.repeat(np.exp2(scales.astype(np.float64) - 127.0), 8, axis=1)[..., None]
    return vals.transpose(0, 1, 3, 2).reshape(g * 512, n)


E2M1 = np.array([0.0, 0.5, 1.0, 1.5, 2.0, 3.0, 4.0, 6.0, -0.0, -0.5, -1.0, -1.5, -2.0, -3.0, -4.0, -6.0])


def pack_fp4(w):
    k, n = w.shape
    w = f64(np.asarray(w, np.float32).astype(ml_dtypes.bfloat16)).reshape(k // 32, 32, n)
    amax = np.abs(w).max(1)
    mant, ex = np.frexp(amax / 6.0)
    byte = np.clip(np.where(amax > 0, np.where(mant > 0.5, ex, ex - 1) + 127, 1), 1, 254)
    scaled = (w * np.exp2(127.0 - byte)[:, None, :]).reshape(k, n).astype(np.float32)
    c = np.ascontiguousarray(scaled.reshape(k // 512, 128, 4, n).transpose(0, 1, 3, 2)).astype(ml_dtypes.float4_e2m1fn).view(np.uint8) & 0xF
    words = (c[..., 0::2] | (c[..., 1::2] << 4)).reshape(k // 512, 128, 2 * n)
    return np.ascontiguousarray(words), np.ascontiguousarray(byte.astype(np.uint8).reshape(k // 512, 16, n))


def unpack_fp4(words, scales):
    g, _, n = scales.shape
    words = np.ascontiguousarray(words).reshape(g, 128, n, 2)
    nib = np.empty((g, 128, n, 4), np.uint8)
    nib[..., 0::2] = words & 0xF
    nib[..., 1::2] = words >> 4
    vals = E2M1[nib] * np.repeat(np.exp2(scales.astype(np.float64) - 127.0), 8, axis=1)[..., None]
    return vals.transpose(0, 1, 3, 2).reshape(g * 512, n)


K, T, S, D, N, H, V, U = 1024, 4096, 1024, 4, 256, 512, 256, 512


def setup_inputs():
    n = np.random.standard_normal
    s = mx_kscale(K)[:, None]
    u = mx_kscale(H)
    packed_xT = pack_weight(n((K, T)) * s)
    packed_w1 = pack_fp4(n((K, H)) / np.sqrt(K) / s)
    packed_w2 = pack_fp4(n((K, H)) / np.sqrt(K) / s)
    packed_w3 = pack_fp4(n((H, N)) / np.sqrt(H) / u[:, None])
    return {
        "x_words": packed_xT[0],
        "x_scales": packed_xT[1],
        "w1_words": packed_w1[0],
        "w1_scales": packed_w1[1],
        "w2_words": packed_w2[0],
        "w2_scales": packed_w2[1],
        "res": (n((H, S))).astype(np.float32),
        "unit": (np.random.uniform(0.6, 1.4, (H, 1)) * u[:, None]).astype(np.float32),
        "w3_words": packed_w3[0],
        "w3_scales": packed_w3[1],
        "offs": striped(np.random.permutation(T)[:S]),
        "lmk": striped(np.random.permutation(np.concatenate([np.arange(V), np.random.randint(0, V, U - V)]))),
    }


def reference(x_words, x_scales, w1_words, w1_scales, w2_words, w2_scales, res, unit, w3_words, w3_scales, offs, lmk):
    xq = unpack_weight(x_words, x_scales)[:, unstriped(offs)]
    jp = unpack_fp4(w2_words, w2_scales).T @ xq
    jd = unpack_fp4(w1_words, w1_scales).T @ xq
    je = jd * f64(res)
    bd = je.reshape(len(je), -1, D).sum(axis=2)
    jj = (jd) ** 2
    hdd = jj.reshape(len(jj), -1, D).sum(axis=2) + 0.5
    ddep = bd / hdd
    red = f64(res) - (jd * np.repeat(ddep, D, axis=1))
    rg = jp * red
    grad = rg.reshape(len(rg), -1, D).sum(axis=2)
    gl = grad[:, unstriped(lmk)]
    dl2 = ddep[:, unstriped(lmk)]
    hid = f64(unit) * (gl * dl2)
    return unpack_fp4(w3_words, w3_scales).T @ mxq(hid, 0, "e4m3")

@@ -1,0 +1,226 @@
+from contextlib import ExitStack
+
+import concourse.mybir as mybir
+from concourse.masks import make_identity
+
+K, T, S, D, N, H, V, U = 1024, 4096, 1024, 4, 256, 512, 256, 512
+FLOPS = 2 * (2 * K * H * S + H * N * U)
+
+F32 = mybir.dt.float32
+BF16 = mybir.dt.bfloat16
+I32 = mybir.dt.int32
+U32 = mybir.dt.uint32
+U16 = mybir.dt.uint16
+U8 = mybir.dt.uint8
+FP8X4 = mybir.dt.float8_e4m3fn_x4
+FP4X4 = mybir.dt.float4_e2m1fn_x4
+ACT = mybir.ActivationFunctionType
+ALU = mybir.AluOpType
+
+P = 128
+PACK = 4
+PASSES = K // (P * PACK)
+BANK = 512
+HALVES = S // BANK
+PTS = BANK // D
+LIST_ROWS = 16
+SLOT_GATHER = 128
+SLOT_HALF = 256
+
+
+def tile_picked_yschur_mul_p_kernel(
+    tc, x_words, x_scales, w1_words, w1_scales, w2_words, w2_scales, res, unit, w3_words, w3_scales, offs, lmk, out
+):
+    nc = tc.nc
+    with ExitStack() as ctx:
+        keep = ctx.enter_context(tc.tile_pool(name="keep", bufs=1))
+        work = ctx.enter_context(tc.tile_pool(name="work", bufs=2))
+        psum = ctx.enter_context(tc.psum_pool(name="psum", bufs=1))
+
+        offs_sb = keep.tile([P, S // LIST_ROWS], U16, name="offs_sb")
+        lmk_sb = keep.tile([P, U // LIST_ROWS], U16, name="lmk_sb")
+        xs_table = keep.tile([P, T], U8, name="xs_table", tag="scales_then_res", align_bytes=64)
+        ws_raw = [keep.tile([P, PASSES, H], U8, name=f"ws_raw{i}", align_bytes=64) for i in range(2)]
+        xs_pass1 = keep.tile([P, S], U8, name="xs_pass1", align_bytes=64)
+        w3s = keep.tile([P, N], U8, name="w3s", align_bytes=64)
+        nc.vector.memset(xs_table[:].bitcast(I32), 0)
+        for i in range(2):
+            nc.gpsimd.memset(ws_raw[i][:].rearrange("p o c -> p (o c)").bitcast(I32), 0)
+        nc.vector.memset(xs_pass1[:].bitcast(I32), 0)
+        nc.vector.memset(w3s[:].bitcast(I32), 0)
+
+        ww_raw = [keep.tile([P, PASSES, 2 * H], U8, name=f"ww_raw{i}", align_bytes=64) for i in range(2)]
+        for i, w_words in enumerate((w1_words, w2_words)):
+            nc.sync.dma_start(ww_raw[i][:].bitcast(I32), w_words.rearrange("o p c -> p o c").bitcast(I32))
+        nc.sync.dma_start(offs_sb[:], offs)
+        for q in range(4):
+            nc.sync.dma_start(
+                xs_table[32 * q : 32 * q + 4 * PASSES, :].bitcast(I32), x_scales[:, 4 * q : 4 * q + 4, :].bitcast(I32)
+            )
+        xw_table = [keep.tile([P, T], U32, name=f"xw_table{o}", align_bytes=64) for o in range(PASSES)]
+
+        def load_scales(i, w_scales, queue):
+            for q in range(4):
+                queue.dma_start(
+                    ws_raw[i][32 * q : 32 * q + 4, :, :].bitcast(I32),
+                    w_scales[:, 4 * q : 4 * q + 4, :].rearrange("o r c -> r o c").bitcast(I32),
+                )
+
+        def load_table(o):
+            nc.sync.dma_start(xw_table[o][:].bitcast(I32), x_words[o].rearrange("p n t -> p (n t)").bitcast(I32))
+
+        load_table(0)
+        load_scales(1, w2_scales, nc.sync)
+        load_table(1)
+        nc.sync.dma_start(lmk_sb[:], lmk)
+
+        ident = keep.tile([P, P], F32, name="ident")
+        load_scales(0, w1_scales, nc.gpsimd)
+        make_identity(nc, ident[:])
+        unit_sb = keep.tile([P, PACK], F32, name="unit_sb")
+        nc.gpsimd.dma_start(unit_sb[:], unit.rearrange("(p t) o -> p (t o)", t=PACK))
+        w3w = keep.tile([P, 2 * N], U8, name="w3w", align_bytes=64)
+        nc.gpsimd.dma_start(w3w[:].bitcast(I32), w3_words[0].bitcast(I32))
+        for q in range(4):
+            nc.gpsimd.dma_start(
+                w3s[32 * q : 32 * q + 4, :].bitcast(I32), w3_scales[0, 4 * q : 4 * q + 4, :].bitcast(I32)
+            )
+
+        ww = [keep.tile([P, PASSES, 2 * H], U8, name=f"ww{i}", align_bytes=64) for i in range(2)]
+        ws = [keep.tile([P, PASSES, H], U8, name=f"ws{i}", align_bytes=64) for i in range(2)]
+
+        def deal_words(i):
+            nc.vector.tensor_copy(
+                ww[i][:].rearrange("p o (t m b) -> p o t m b", t=PACK, b=2),
+                ww_raw[i][:].rearrange("p o (m t b) -> p o t m b", t=PACK, b=2),
+            )
+
+        def deal_scales(i):
+            nc.vector.tensor_copy(
+                ws[i][:].rearrange("p o (t m) -> p o t m", t=PACK),
+                ws_raw[i][:].rearrange("p o (m t) -> p o t m", t=PACK),
+            )
+
+        xs_picked = keep.tile([P, S], U8, name="xs_picked", align_bytes=64)
+        xw = [[keep.tile([P, BANK], U32, name=f"xw{o}_{h}", align_bytes=64) for h in range(HALVES)] for o in range(PASSES)]
+
+        def gather_words(o, h):
+            cols = BANK // LIST_ROWS
+            nc.vector.tensor_copy(xw[o][h][:], xw_table[o][:].indirect(offs_sb[:, h * cols : (h + 1) * cols]))
+
+        deal_words(0)
+        nc.vector.tensor_copy(xs_picked[:], xs_table[:].indirect(offs_sb[:]))
+        for q in range(4):
+            nc.sync.dma_start(
+                xs_pass1[32 * q : 32 * q + 4, :].bitcast(I32), xs_picked[32 * q + 4 : 32 * q + 8, :].bitcast(I32)
+            )
+        res_rows = res.rearrange("(p t) s -> p t s", t=PACK)
+        res_sb = keep.tile([P, PACK, S], F32, name="res_sb", tag="scales_then_res", align_bytes=64)
+        for t in range(PACK):
+            nc.sync.dma_start(res_sb[:, t, :], res_rows[:, t, :])
+        deal_words(1)
+        for h in range(HALVES):
+            gather_words(0, h)
+        for i in range(2):
+            deal_scales(i)
+        for h in range(HALVES):
+            gather_words(1, h)
+        xs = (xs_picked, xs_pass1)
+
+        planes = keep.tile([P, PACK, U], BF16, name="planes", align_bytes=64)
+
+        def product(acc, i, t, h):
+            for o in range(PASSES):
+                nc.tensor.matmul_mx(
+                    acc[:],
+                    lhsT=ww[i][:, o, 2 * P * t : 2 * P * (t + 1)].bitcast(FP4X4),
+                    lhsT_scale=ws[i][:, o, P * t : P * (t + 1)],
+                    rhs=xw[o][h][:].bitcast(FP8X4),
+                    rhs_scale=xs[o][:, BANK * h : BANK * (h + 1)],
+                    start=(o == 0),
+                    stop=(o == PASSES - 1),
+                )
+
+        def point_sums(sums, terms):
+            for d in range(D):
+                nc.tensor.matmul(sums, lhsT=terms[:, d, :], rhs=ident[:], is_transpose=True, start=(d == 0), stop=(d == D - 1))
+
+        for t in range(PACK):
+            ab = psum.tile([P, 2, HALVES, P], F32, name="ab", bufs=1)
+            ce = psum.tile([P, 2, HALVES, P], F32, name="ce", bufs=2)
+            for h in range(HALVES):
+                jd = psum.tile([P, BANK], F32, name="jd", bufs=2)
+                jp = psum.tile([P, BANK], F32, name="jp", bufs=2)
+                product(jd, 0, t, h)
+                product(jp, 1, t, h)
+                r_vd = res_sb[:, t, BANK * h : BANK * (h + 1)].rearrange("p (v d) -> p v d", d=D)
+                jd_res = work.tile([P, D, PTS], F32, name="jd_res")
+                jd_sb = work.tile([P, D, PTS], F32, name="jd_sb")
+                jd_sq = work.tile([P, D, PTS], F32, name="jd_sq")
+                jp_res = work.tile([P, D, PTS], F32, name="jp_res")
+                jp_jd = work.tile([P, D, PTS], F32, name="jp_jd")
+                nc.vector.tensor_tensor(
+                    jd_res[:].rearrange("p d v -> p v d"), jd[:].rearrange("p (v d) -> p v d", d=D), r_vd, ALU.mult
+                )
+                nc.scalar.activation(jd_sq[:], jd[:].rearrange("p (v d) -> p d v", d=D), ACT.Square)
+                nc.scalar.copy(jd_sb[:], jd[:].rearrange("p (v d) -> p d v", d=D))
+                nc.vector.tensor_tensor(
+                    jp_res[:].rearrange("p d v -> p v d"), jp[:].rearrange("p (v d) -> p v d", d=D), r_vd, ALU.mult
+                )
+                nc.vector.tensor_tensor(jp_jd[:], jp[:].rearrange("p (v d) -> p d v", d=D), jd_sb[:], ALU.mult)
+                point_sums(ab[:, 0, h, :], jd_res)
+                point_sums(ab[:, 1, h, :], jd_sq)
+                point_sums(ce[:, 0, h, :], jp_res)
+                point_sums(ce[:, 1, h, :], jp_jd)
+
+            root = work.tile([P, HALVES, P], F32, name="root")
+            inv = work.tile([P, HALVES, P], F32, name="inv")
+            ddep = work.tile([P, HALVES, P], F32, name="ddep")
+            taken = work.tile([P, HALVES, P], F32, name="taken")
+            grad = work.tile([P, HALVES, P], F32, name="grad")
+            both = work.tile([P, HALVES, P], F32, name="both")
+            nc.scalar.activation(root[:], ab[:, 1, :, :], ACT.Abs_reciprocal_sqrt, bias=0.5)
+            nc.scalar.activation(inv[:], root[:], ACT.Square)
+            nc.vector.tensor_tensor(ddep[:], ab[:, 0, :, :], inv[:], ALU.mult)
+            nc.vector.tensor_tensor(taken[:], ce[:, 1, :, :], ddep[:], ALU.mult)
+            nc.vector.tensor_tensor(grad[:], ce[:, 0, :, :], taken[:], ALU.subtract)
+            nc.vector.tensor_tensor(both[:], grad[:], ddep[:], ALU.mult)
+            back = psum.tile([P, HALVES, PTS], F32, name="back", bufs=1)
+            for h in range(HALVES):
+                nc.tensor.transpose(back[:, h, :], both[:, h, :], ident[:])
+            table = work.tile([P, V], F32, name="table")
+            nc.scalar.activation(table[:], back[:].rearrange("p h v -> p (h v)"), ACT.Copy, scale=unit_sb[:, t : t + 1])
+            for c in range(U // SLOT_GATHER):
+                cols = SLOT_GATHER // LIST_ROWS
+                picked = table[:].indirect(lmk_sb[:, c * cols : (c + 1) * cols])
+                dst = planes[:, t, c * SLOT_GATHER : (c + 1) * SLOT_GATHER]
+                if t == PACK - 1 and c < 2:
+                    nc.vector.tensor_copy(dst, picked)
+                else:
+                    nc.scalar.activation(dst, picked, ACT.Copy)
+
+        out_rows = out.rearrange("(m p) r -> p m r", p=P)
+        for s in range(U // SLOT_HALF):
+            slots = slice(s * SLOT_HALF, (s + 1) * SLOT_HALF)
+            hid = work.tile([P, SLOT_HALF, PACK], BF16, name="hid", align_bytes=64)
+            nc.vector.tensor_copy(hid[:], planes[:, :, slots].rearrange("p t r -> p r t"))
+            hw = work.tile([P, SLOT_HALF], U32, name="hw", align_bytes=64)
+            hs = work.tile([P, SLOT_HALF], U8, name="hs", align_bytes=64)
+            nc.vector.quantize_mx(hw[:].bitcast(FP8X4), hs[:], hid[:].rearrange("p r t -> p (r t)"))
+            staged = work.tile([P, N // P, SLOT_HALF], F32, name="staged")
+            for m in range(N // P):
+                acc = psum.tile([P, BANK], F32, name=("jd", "jp")[m], bufs=2)
+                nc.tensor.matmul_mx(
+                    acc[:, :SLOT_HALF],
+                    lhsT=w3w[:, 2 * P * m : 2 * P * (m + 1)].bitcast(FP4X4),
+                    lhsT_scale=w3s[:, P * m : P * (m + 1)],
+                    rhs=hw[:].bitcast(FP8X4),
+                    rhs_scale=hs[:],
+                    start=True,
+                    stop=True,
+                )
+                if m == 0:
+                    nc.scalar.copy(staged[:, m, :], acc[:, :SLOT_HALF])
+                else:
+                    nc.vector.tensor_copy(staged[:, m, :], acc[:, :SLOT_HALF])
+            nc.sync.dma_start(out_rows[:, :, slots], staged[:])

@@ -39,25 +39,20 @@ def tile_picked_yschur_mul_p_kernel(
 
         offs_sb = keep.tile([P, S // LIST_ROWS], U16, name="offs_sb")
         lmk_sb = keep.tile([P, U // LIST_ROWS], U16, name="lmk_sb")
-        xs_table = keep.tile([P, T], U8, name="xs_table", tag="scales_then_res", align_bytes=64)
+        xs_table = keep.tile([P, T], U8, name="xs_table", tag="scale_table", align_bytes=64)
         ws_raw = [keep.tile([P, PASSES, H], U8, name=f"ws_raw{i}", align_bytes=64) for i in range(2)]
-        xs_pass1 = keep.tile([P, S], U8, name="xs_pass1", align_bytes=64)
-        w3s = keep.tile([P, N], U8, name="w3s", align_bytes=64)
+        xs = keep.tile([P, PASSES, S], U8, name="xs", align_bytes=64)
         nc.vector.memset(xs_table[:].bitcast(I32), 0)
         for i in range(2):
             nc.gpsimd.memset(ws_raw[i][:].rearrange("p o c -> p (o c)").bitcast(I32), 0)
-        nc.vector.memset(xs_pass1[:].bitcast(I32), 0)
-        nc.vector.memset(w3s[:].bitcast(I32), 0)
+        nc.vector.memset(xs[:].rearrange("p o s -> p (o s)").bitcast(I32), 0)
 
-        ww_raw = [keep.tile([P, PASSES, 2 * H], U8, name=f"ww_raw{i}", align_bytes=64) for i in range(2)]
+        ww_raw = [keep.tile([P, PASSES, 2 * H], U8, name=f"ww_raw{i}", tag=f"raw_words{i}", align_bytes=64) for i in range(2)]
         for i, w_words in enumerate((w1_words, w2_words)):
             nc.sync.dma_start(ww_raw[i][:].bitcast(I32), w_words.rearrange("o p c -> p o c").bitcast(I32))
         nc.sync.dma_start(offs_sb[:], offs)
-        for q in range(4):
-            nc.sync.dma_start(
-                xs_table[32 * q : 32 * q + 4 * PASSES, :].bitcast(I32), x_scales[:, 4 * q : 4 * q + 4, :].bitcast(I32)
-            )
-        xw_table = [keep.tile([P, T], U32, name=f"xw_table{o}", align_bytes=64) for o in range(PASSES)]
+        nc.scalar.dma_start(xs_table[0:P:4, :].bitcast(I32), x_scales.rearrange("o r c -> (o r) c").bitcast(I32))
+        xw_table = []
 
         def load_scales(i, w_scales, queue):
             for q in range(4):
@@ -66,25 +61,17 @@ def tile_picked_yschur_mul_p_kernel(
                     w_scales[:, 4 * q : 4 * q + 4, :].rearrange("o r c -> r o c").bitcast(I32),
                 )
 
-        def load_table(o):
+        def load_table(o, tag):
+            xw_table.append(keep.tile([P, T], U32, name=f"xw_table{o}", tag=tag, align_bytes=64))
             nc.sync.dma_start(xw_table[o][:].bitcast(I32), x_words[o].rearrange("p n t -> p (n t)").bitcast(I32))
 
-        load_table(0)
-        load_scales(1, w2_scales, nc.sync)
-        load_table(1)
+        load_table(0, "table0")
+        load_scales(1, w2_scales, nc.scalar)
         nc.sync.dma_start(lmk_sb[:], lmk)
 
         ident = keep.tile([P, P], F32, name="ident")
         load_scales(0, w1_scales, nc.gpsimd)
         make_identity(nc, ident[:])
-        unit_sb = keep.tile([P, PACK], F32, name="unit_sb")
-        nc.gpsimd.dma_start(unit_sb[:], unit.rearrange("(p t) o -> p (t o)", t=PACK))
-        w3w = keep.tile([P, 2 * N], U8, name="w3w", align_bytes=64)
-        nc.gpsimd.dma_start(w3w[:].bitcast(I32), w3_words[0].bitcast(I32))
-        for q in range(4):
-            nc.gpsimd.dma_start(
-                w3s[32 * q : 32 * q + 4, :].bitcast(I32), w3_scales[0, 4 * q : 4 * q + 4, :].bitcast(I32)
-            )
 
         ww = [keep.tile([P, PASSES, 2 * H], U8, name=f"ww{i}", align_bytes=64) for i in range(2)]
         ws = [keep.tile([P, PASSES, H], U8, name=f"ws{i}", align_bytes=64) for i in range(2)]
@@ -101,7 +88,7 @@ def tile_picked_yschur_mul_p_kernel(
                 ws_raw[i][:].rearrange("p o (m t) -> p o t m", t=PACK),
             )
 
-        xs_picked = keep.tile([P, S], U8, name="xs_picked", align_bytes=64)
+        xs_picked = keep.tile([P, S], U8, name="xs_picked", tag="scales_then_res", align_bytes=64)
         xw = [[keep.tile([P, BANK], U32, name=f"xw{o}_{h}", align_bytes=64) for h in range(HALVES)] for o in range(PASSES)]
 
         def gather_words(o, h):
@@ -109,11 +96,17 @@ def tile_picked_yschur_mul_p_kernel(
             nc.vector.tensor_copy(xw[o][h][:], xw_table[o][:].indirect(offs_sb[:, h * cols : (h + 1) * cols]))
 
         deal_words(0)
+        load_table(1, "raw_words0")
         nc.vector.tensor_copy(xs_picked[:], xs_table[:].indirect(offs_sb[:]))
-        for q in range(4):
-            nc.sync.dma_start(
-                xs_pass1[32 * q : 32 * q + 4, :].bitcast(I32), xs_picked[32 * q + 4 : 32 * q + 8, :].bitcast(I32)
-            )
+        for o in range(PASSES):
+            for q in range(4):
+                first = 64 * o + 16 * q
+                queue = nc.gpsimd if (o, q) == (0, 0) else nc.scalar
+                queue.dma_start(
+                    xs[32 * q : 32 * q + 4, o, :].bitcast(I32), xs_picked[first : first + 16 : 4, :].bitcast(I32)
+                )
+        unit_sb = keep.tile([P, PACK], F32, name="unit_sb", tag="scale_table", align_bytes=64)
+        nc.gpsimd.dma_start(unit_sb[:], unit.rearrange("(p t) o -> p (t o)", t=PACK))
         res_rows = res.rearrange("(p t) s -> p t s", t=PACK)
         res_sb = keep.tile([P, PACK, S], F32, name="res_sb", tag="scales_then_res", align_bytes=64)
         for t in range(PACK):
@@ -125,7 +118,13 @@ def tile_picked_yschur_mul_p_kernel(
             deal_scales(i)
         for h in range(HALVES):
             gather_words(1, h)
-        xs = (xs_picked, xs_pass1)
+
+        w3w = keep.tile([P, 2 * N], U8, name="w3w", tag="table0", align_bytes=64)
+        nc.sync.dma_start(w3w[:].bitcast(I32), w3_words[0].bitcast(I32))
+        w3s = keep.tile([P, N], U8, name="w3s", tag="raw_words0", align_bytes=64)
+        nc.gpsimd.memset(w3s[:].bitcast(I32), 0)
+        for q in range(4):
+            nc.sync.dma_start(w3s[32 * q : 32 * q + 4, :].bitcast(I32), w3_scales[0, 4 * q : 4 * q + 4, :].bitcast(I32))
 
         planes = keep.tile([P, PACK, U], BF16, name="planes", align_bytes=64)
 
@@ -136,68 +135,117 @@ def tile_picked_yschur_mul_p_kernel(
                     lhsT=ww[i][:, o, 2 * P * t : 2 * P * (t + 1)].bitcast(FP4X4),
                     lhsT_scale=ws[i][:, o, P * t : P * (t + 1)],
                     rhs=xw[o][h][:].bitcast(FP8X4),
-                    rhs_scale=xs[o][:, BANK * h : BANK * (h + 1)],
+                    rhs_scale=xs[:, o, BANK * h : BANK * (h + 1)],
                     start=(o == 0),
                     stop=(o == PASSES - 1),
                 )
 
         def point_sums(sums, terms):
-            for d in range(D):
-                nc.tensor.matmul(sums, lhsT=terms[:, d, :], rhs=ident[:], is_transpose=True, start=(d == 0), stop=(d == D - 1))
-
-        for t in range(PACK):
-            ab = psum.tile([P, 2, HALVES, P], F32, name="ab", bufs=1)
-            ce = psum.tile([P, 2, HALVES, P], F32, name="ce", bufs=2)
-            for h in range(HALVES):
-                jd = psum.tile([P, BANK], F32, name="jd", bufs=2)
-                jp = psum.tile([P, BANK], F32, name="jp", bufs=2)
-                product(jd, 0, t, h)
-                product(jp, 1, t, h)
-                r_vd = res_sb[:, t, BANK * h : BANK * (h + 1)].rearrange("p (v d) -> p v d", d=D)
-                jd_res = work.tile([P, D, PTS], F32, name="jd_res")
-                jd_sb = work.tile([P, D, PTS], F32, name="jd_sb")
-                jd_sq = work.tile([P, D, PTS], F32, name="jd_sq")
-                jp_res = work.tile([P, D, PTS], F32, name="jp_res")
-                jp_jd = work.tile([P, D, PTS], F32, name="jp_jd")
-                nc.vector.tensor_tensor(
-                    jd_res[:].rearrange("p d v -> p v d"), jd[:].rearrange("p (v d) -> p v d", d=D), r_vd, ALU.mult
+            count = terms.shape[1]
+            for d in range(count):
+                nc.tensor.matmul(
+                    sums, lhsT=terms[:, d, :], rhs=ident[:], is_transpose=True, start=(d == 0), stop=(d == count - 1)
                 )
-                nc.scalar.activation(jd_sq[:], jd[:].rearrange("p (v d) -> p d v", d=D), ACT.Square)
-                nc.scalar.copy(jd_sb[:], jd[:].rearrange("p (v d) -> p d v", d=D))
-                nc.vector.tensor_tensor(
-                    jp_res[:].rearrange("p d v -> p v d"), jp[:].rearrange("p (v d) -> p v d", d=D), r_vd, ALU.mult
-                )
-                nc.vector.tensor_tensor(jp_jd[:], jp[:].rearrange("p (v d) -> p d v", d=D), jd_sb[:], ALU.mult)
-                point_sums(ab[:, 0, h, :], jd_res)
-                point_sums(ab[:, 1, h, :], jd_sq)
-                point_sums(ce[:, 0, h, :], jp_res)
-                point_sums(ce[:, 1, h, :], jp_jd)
 
-            root = work.tile([P, HALVES, P], F32, name="root")
-            inv = work.tile([P, HALVES, P], F32, name="inv")
-            ddep = work.tile([P, HALVES, P], F32, name="ddep")
-            taken = work.tile([P, HALVES, P], F32, name="taken")
-            grad = work.tile([P, HALVES, P], F32, name="grad")
-            both = work.tile([P, HALVES, P], F32, name="both")
-            nc.scalar.activation(root[:], ab[:, 1, :, :], ACT.Abs_reciprocal_sqrt, bias=0.5)
+        def by_member(cols):
+            return cols.rearrange("p (v d) -> p d v", d=D)
+
+        def prepare(t, h):
+            res_dv = work.tile([P, D, PTS], F32, name="res_dv", bufs=3)
+            nc.gpsimd.tensor_copy(res_dv[:], by_member(res_sb[:, t, BANK * h : BANK * (h + 1)]))
+            jd = psum.tile([P, BANK], F32, name="jd", tag="product", bufs=3)
+            product(jd, 0, t, h)
+            jp = psum.tile([P, BANK], F32, name="jp", tag="product", bufs=3)
+            product(jp, 1, t, h)
+            return res_dv, jd, jp
+
+        def multiply(res_dv, jd, jp):
+            depth = work.tile([P, 2, D, PTS], F32, name="depth")
+            jd_sb = work.tile([P, D, PTS], F32, name="jd_sb")
+            pose = work.tile([P, 2, D, PTS], F32, name="pose")
+            nc.scalar.copy(jd_sb[:], by_member(jd[:]))
+            nc.vector.tensor_tensor(depth[:, 0, :, :], by_member(jd[:]), res_dv[:], ALU.mult)
+            nc.scalar.activation(depth[:, 1, :, :], jd_sb[:], ACT.Square)
+            nc.vector.tensor_tensor(pose[:, 0, :, :], by_member(jp[:]), res_dv[:], ALU.mult)
+            nc.vector.tensor_tensor(pose[:, 1, :, :], by_member(jp[:]), jd_sb[:], ALU.mult)
+            return depth, pose
+
+        def add_up(depth, pose, depth_sums, pose_sums, fold):
+            if fold:
+                folded = work.tile([P, 2, D // 2, PTS], F32, name="folded")
+                nc.gpsimd.tensor_tensor(folded[:], depth[:, :, : D // 2, :], depth[:, :, D // 2 :, :], ALU.add)
+                depth = folded
+            order = ((pose, pose_sums), (depth, depth_sums)) if fold else ((depth, depth_sums), (pose, pose_sums))
+            for terms, sums in order:
+                for i in range(2):
+                    point_sums(sums[:, i, :], terms[:, i, :, :])
+
+        def eliminate(depth_sums, pose_sums, both):
+            shape = list(both.shape)
+            root = work.tile(shape, F32, name="root")
+            inv = work.tile(shape, F32, name="inv")
+            ddep = work.tile(shape, F32, name="ddep")
+            taken = work.tile(shape, F32, name="taken")
+            grad = work.tile(shape, F32, name="grad")
+            nc.scalar.activation(root[:], depth_sums[:, 1, :], ACT.Abs_reciprocal_sqrt, bias=0.5)
             nc.scalar.activation(inv[:], root[:], ACT.Square)
-            nc.vector.tensor_tensor(ddep[:], ab[:, 0, :, :], inv[:], ALU.mult)
-            nc.vector.tensor_tensor(taken[:], ce[:, 1, :, :], ddep[:], ALU.mult)
-            nc.vector.tensor_tensor(grad[:], ce[:, 0, :, :], taken[:], ALU.subtract)
-            nc.vector.tensor_tensor(both[:], grad[:], ddep[:], ALU.mult)
-            back = psum.tile([P, HALVES, PTS], F32, name="back", bufs=1)
+            nc.vector.tensor_tensor(ddep[:], depth_sums[:, 0, :], inv[:], ALU.mult)
+            nc.vector.tensor_tensor(taken[:], pose_sums[:, 1, :], ddep[:], ALU.mult)
+            nc.vector.tensor_tensor(grad[:], pose_sums[:, 0, :], taken[:], ALU.subtract)
+            nc.vector.tensor_tensor(both, grad[:], ddep[:], ALU.mult)
+
+        def make_table(t, both):
+            back = psum.tile([P, V], F32, name="back", bufs=1)
             for h in range(HALVES):
-                nc.tensor.transpose(back[:, h, :], both[:, h, :], ident[:])
+                nc.tensor.transpose(back[:, h * PTS : (h + 1) * PTS], both[:, h * P : (h + 1) * P], ident[:])
             table = work.tile([P, V], F32, name="table")
-            nc.scalar.activation(table[:], back[:].rearrange("p h v -> p (h v)"), ACT.Copy, scale=unit_sb[:, t : t + 1])
+            nc.scalar.activation(table[:], back[:], ACT.Copy, scale=unit_sb[:, t : t + 1])
+            return table
+
+        def look_up(t, table, on_vector):
+            cols = SLOT_GATHER // LIST_ROWS
             for c in range(U // SLOT_GATHER):
-                cols = SLOT_GATHER // LIST_ROWS
                 picked = table[:].indirect(lmk_sb[:, c * cols : (c + 1) * cols])
                 dst = planes[:, t, c * SLOT_GATHER : (c + 1) * SLOT_GATHER]
-                if t == PACK - 1 and c < 2:
+                if c < on_vector:
                     nc.vector.tensor_copy(dst, picked)
                 else:
                     nc.scalar.activation(dst, picked, ACT.Copy)
+
+        def sum_banks(width):
+            depth_sums = psum.tile([P, 2, width], F32, name="depth_sums", bufs=2)
+            pose_sums = psum.tile([P, 2, width], F32, name="pose_sums", bufs=2)
+            return depth_sums, pose_sums
+
+        units = [(t, h) for t in range(PACK) for h in range(HALVES)]
+        last = PACK - 1
+        sums, both, tables = {}, {}, {}
+        ready = prepare(*units[0])
+        for u, (t, h) in enumerate(units):
+            current = ready
+            if u + 1 < len(units):
+                ready = prepare(*units[u + 1])
+            depth, pose = multiply(*current)
+            if h == 0:
+                both[t] = work.tile([P, HALVES * P], F32, name="both")
+            if t < last:
+                if h == 0:
+                    sums[t] = sum_banks(HALVES * P)
+                cols = slice(h * P, (h + 1) * P)
+                add_up(depth, pose, sums[t][0][:, :, cols], sums[t][1][:, :, cols], True)
+            else:
+                sums[t, h] = sum_banks(P)
+                add_up(depth, pose, sums[t, h][0][:], sums[t, h][1][:], h == 0)
+            if t > 0 and h == 0:
+                eliminate(sums[t - 1][0][:], sums[t - 1][1][:], both[t - 1][:])
+                if t > 1:
+                    look_up(t - 2, tables[t - 2], 0)
+            if t > 0 and h == 1:
+                tables[t - 1] = make_table(t - 1, both[t - 1])
+        for h in range(HALVES):
+            eliminate(sums[last, h][0][:], sums[last, h][1][:], both[last][:, h * P : (h + 1) * P])
+        look_up(last - 1, tables[last - 1], 0)
+        look_up(last, make_table(last, both[last]), 2)
 
         out_rows = out.rearrange("(m p) r -> p m r", p=P)
         for s in range(U // SLOT_HALF):
@@ -209,7 +257,7 @@ def tile_picked_yschur_mul_p_kernel(
             nc.vector.quantize_mx(hw[:].bitcast(FP8X4), hs[:], hid[:].rearrange("p r t -> p (r t)"))
             staged = work.tile([P, N // P, SLOT_HALF], F32, name="staged")
             for m in range(N // P):
-                acc = psum.tile([P, BANK], F32, name=("jd", "jp")[m], bufs=2)
+                acc = psum.tile([P, BANK], F32, name="acc", tag="product", bufs=3)
                 nc.tensor.matmul_mx(
                     acc[:, :SLOT_HALF],
                     lhsT=w3w[:, 2 * P * m : 2 * P * (m + 1)].bitcast(FP4X4),

@@ -26,6 +26,11 @@ PTS = BANK // D
 LIST_ROWS = 16
 SLOT_GATHER = 128
 SLOT_HALF = 256
+SCALE_ROWS = 16
+COPIES = P // (PASSES * SCALE_ROWS)
+PLANE = S + 2 * H
+TABLE_BYTES = 4 * T
+X_SCALES_AT = 2 * TABLE_BYTES
 
 
 def tile_picked_yschur_mul_p_kernel(
@@ -35,93 +40,92 @@ def tile_picked_yschur_mul_p_kernel(
     with ExitStack() as ctx:
         keep = ctx.enter_context(tc.tile_pool(name="keep", bufs=1))
         work = ctx.enter_context(tc.tile_pool(name="work", bufs=2))
+        shared = ctx.enter_context(tc.tile_pool(name="shared", bufs=1))
         psum = ctx.enter_context(tc.psum_pool(name="psum", bufs=1))
 
         offs_sb = keep.tile([P, S // LIST_ROWS], U16, name="offs_sb")
         lmk_sb = keep.tile([P, U // LIST_ROWS], U16, name="lmk_sb")
-        xs_table = keep.tile([P, T], U8, name="xs_table", tag="scale_table", align_bytes=64)
-        ws_raw = [keep.tile([P, PASSES, H], U8, name=f"ws_raw{i}", align_bytes=64) for i in range(2)]
-        xs = keep.tile([P, PASSES, S], U8, name="xs", align_bytes=64)
-        nc.vector.memset(xs_table[:].bitcast(I32), 0)
-        for i in range(2):
-            nc.gpsimd.memset(ws_raw[i][:].rearrange("p o c -> p (o c)").bitcast(I32), 0)
-        nc.vector.memset(xs[:].rearrange("p o s -> p (o s)").bitcast(I32), 0)
+        unit_sb = keep.tile([P, PACK], F32, name="unit_sb")
+        nc.sync.dma_start(offs_sb[:], offs)
+        nc.sync.dma_start(lmk_sb[:], lmk)
+        nc.sync.dma_start(unit_sb[:], unit.rearrange("(p t) o -> p (t o)", t=PACK))
 
-        ww_raw = [keep.tile([P, PASSES, 2 * H], U8, name=f"ww_raw{i}", tag=f"raw_words{i}", align_bytes=64) for i in range(2)]
+        def load_scale_rows(dst, scales):
+            rows = scales.rearrange("o r c -> (o r) c").bitcast(I32)
+            nc.sync.dma_start(dst.bitcast(I32), rows.unsqueeze(1).to_broadcast([rows.shape[0], COPIES, rows.shape[1]]))
+
+        xs_table = shared.tile([P, T], U8, name="xs_table", align_bytes=64, offset=X_SCALES_AT)
+        load_scale_rows(xs_table[:], x_scales)
+        ws_raw = keep.tile([P, 2, H], U8, name="ws_raw", align_bytes=64)
+        for i, w_scales in enumerate((w1_scales, w2_scales)):
+            load_scale_rows(ws_raw[:, i, :], w_scales)
+        ww_raw = [keep.tile([P, PASSES, 2 * H], U8, name=f"ww_raw{i}", align_bytes=64) for i in range(2)]
         for i, w_words in enumerate((w1_words, w2_words)):
             nc.sync.dma_start(ww_raw[i][:].bitcast(I32), w_words.rearrange("o p c -> p o c").bitcast(I32))
-        nc.sync.dma_start(offs_sb[:], offs)
-        nc.scalar.dma_start(xs_table[0:P:4, :].bitcast(I32), x_scales.rearrange("o r c -> (o r) c").bitcast(I32))
         xw_table = []
 
-        def load_scales(i, w_scales, queue):
-            for q in range(4):
-                queue.dma_start(
-                    ws_raw[i][32 * q : 32 * q + 4, :, :].bitcast(I32),
-                    w_scales[:, 4 * q : 4 * q + 4, :].rearrange("o r c -> r o c").bitcast(I32),
-                )
-
-        def load_table(o, tag):
-            xw_table.append(keep.tile([P, T], U32, name=f"xw_table{o}", tag=tag, align_bytes=64))
+        def load_table(o):
+            xw_table.append(shared.tile([P, T], U32, name=f"xw_table{o}", align_bytes=64, offset=o * TABLE_BYTES))
             nc.sync.dma_start(xw_table[o][:].bitcast(I32), x_words[o].rearrange("p n t -> p (n t)").bitcast(I32))
 
-        load_table(0, "table0")
-        load_scales(1, w2_scales, nc.scalar)
-        nc.sync.dma_start(lmk_sb[:], lmk)
+        load_table(0)
 
+        plane = [keep.tile([P, PLANE], U8, name=f"plane{o}", align_bytes=64) for o in range(PASSES)]
+        for o in range(PASSES):
+            nc.vector.memset(plane[o][:].bitcast(I32), 0)
         ident = keep.tile([P, P], F32, name="ident")
-        load_scales(0, w1_scales, nc.gpsimd)
         make_identity(nc, ident[:])
 
-        ww = [keep.tile([P, PASSES, 2 * H], U8, name=f"ww{i}", align_bytes=64) for i in range(2)]
-        ws = [keep.tile([P, PASSES, H], U8, name=f"ws{i}", align_bytes=64) for i in range(2)]
+        xs_picked = shared.tile([P, S], U8, name="xs_picked", align_bytes=64, offset=TABLE_BYTES)
+        scale_rows = keep.tile([P, PLANE], U8, name="scale_rows", align_bytes=64)
+        nc.vector.tensor_copy(xs_picked[:], xs_table[:].indirect(offs_sb[:]))
+        nc.vector.tensor_copy(
+            scale_rows[:, S:].rearrange("p (i t m) -> p i t m", i=2, t=PACK),
+            ws_raw[:].rearrange("p i (m t) -> p i t m", t=PACK),
+        )
+        nc.vector.tensor_copy(scale_rows[:, :S].bitcast(I32), xs_picked[:].bitcast(I32))
 
-        def deal_words(i):
+        def place_scales(o):
+            for q in range(4):
+                first = COPIES * (SCALE_ROWS * o + 4 * q)
+                nc.sync.dma_start(
+                    plane[o][32 * q : 32 * q + 4, :].bitcast(I32),
+                    scale_rows[first : first + 4 * COPIES : COPIES, :].bitcast(I32),
+                )
+
+        place_scales(0)
+        load_table(1)
+        place_scales(1)
+
+        ww = []
+        for i in range(2):
+            ww.append(
+                shared.tile(
+                    [P, PASSES, 2 * H], U8, name=f"ww{i}", align_bytes=64, offset=X_SCALES_AT + i * PASSES * 2 * H
+                )
+            )
             nc.vector.tensor_copy(
                 ww[i][:].rearrange("p o (t m b) -> p o t m b", t=PACK, b=2),
                 ww_raw[i][:].rearrange("p o (m t b) -> p o t m b", t=PACK, b=2),
             )
 
-        def deal_scales(i):
-            nc.vector.tensor_copy(
-                ws[i][:].rearrange("p o (t m) -> p o t m", t=PACK),
-                ws_raw[i][:].rearrange("p o (m t) -> p o t m", t=PACK),
-            )
-
-        xs_picked = keep.tile([P, S], U8, name="xs_picked", tag="scales_then_res", align_bytes=64)
         xw = [[keep.tile([P, BANK], U32, name=f"xw{o}_{h}", align_bytes=64) for h in range(HALVES)] for o in range(PASSES)]
 
-        def gather_words(o, h):
+        def gather_words(o):
             cols = BANK // LIST_ROWS
-            nc.vector.tensor_copy(xw[o][h][:], xw_table[o][:].indirect(offs_sb[:, h * cols : (h + 1) * cols]))
+            for h in range(HALVES):
+                nc.vector.tensor_copy(xw[o][h][:], xw_table[o][:].indirect(offs_sb[:, h * cols : (h + 1) * cols]))
 
-        deal_words(0)
-        load_table(1, "raw_words0")
-        nc.vector.tensor_copy(xs_picked[:], xs_table[:].indirect(offs_sb[:]))
-        for o in range(PASSES):
-            for q in range(4):
-                first = 64 * o + 16 * q
-                queue = nc.gpsimd if (o, q) == (0, 0) else nc.scalar
-                queue.dma_start(
-                    xs[32 * q : 32 * q + 4, o, :].bitcast(I32), xs_picked[first : first + 16 : 4, :].bitcast(I32)
-                )
-        unit_sb = keep.tile([P, PACK], F32, name="unit_sb", tag="scale_table", align_bytes=64)
-        nc.gpsimd.dma_start(unit_sb[:], unit.rearrange("(p t) o -> p (t o)", t=PACK))
+        gather_words(0)
         res_rows = res.rearrange("(p t) s -> p t s", t=PACK)
-        res_sb = keep.tile([P, PACK, S], F32, name="res_sb", tag="scales_then_res", align_bytes=64)
+        res_sb = shared.tile([P, PACK, S], F32, name="res_sb", align_bytes=64, offset=0)
         for t in range(PACK):
             nc.sync.dma_start(res_sb[:, t, :], res_rows[:, t, :])
-        deal_words(1)
-        for h in range(HALVES):
-            gather_words(0, h)
-        for i in range(2):
-            deal_scales(i)
-        for h in range(HALVES):
-            gather_words(1, h)
+        gather_words(1)
 
-        w3w = keep.tile([P, 2 * N], U8, name="w3w", tag="table0", align_bytes=64)
+        w3w = shared.tile([P, 2 * N], U8, name="w3w", align_bytes=64, offset=TABLE_BYTES)
         nc.sync.dma_start(w3w[:].bitcast(I32), w3_words[0].bitcast(I32))
-        w3s = keep.tile([P, N], U8, name="w3s", tag="raw_words0", align_bytes=64)
+        w3s = shared.tile([P, N], U8, name="w3s", align_bytes=64, offset=TABLE_BYTES + 2 * N)
         nc.gpsimd.memset(w3s[:].bitcast(I32), 0)
         for q in range(4):
             nc.sync.dma_start(w3s[32 * q : 32 * q + 4, :].bitcast(I32), w3_scales[0, 4 * q : 4 * q + 4, :].bitcast(I32))
@@ -133,9 +137,9 @@ def tile_picked_yschur_mul_p_kernel(
                 nc.tensor.matmul_mx(
                     acc[:],
                     lhsT=ww[i][:, o, 2 * P * t : 2 * P * (t + 1)].bitcast(FP4X4),
-                    lhsT_scale=ws[i][:, o, P * t : P * (t + 1)],
+                    lhsT_scale=plane[o][:, S + H * i + P * t : S + H * i + P * (t + 1)],
                     rhs=xw[o][h][:].bitcast(FP8X4),
-                    rhs_scale=xs[:, o, BANK * h : BANK * (h + 1)],
+                    rhs_scale=plane[o][:, BANK * h : BANK * (h + 1)],
                     start=(o == 0),
                     stop=(o == PASSES - 1),
                 )
@@ -180,27 +184,27 @@ def tile_picked_yschur_mul_p_kernel(
                 for i in range(2):
                     point_sums(sums[:, i, :], terms[:, i, :, :])
 
-        def eliminate(depth_sums, pose_sums, both):
-            shape = list(both.shape)
+        def eliminate(depth_sums, pose_sums):
+            shape = [P, depth_sums.shape[2]]
             root = work.tile(shape, F32, name="root")
             inv = work.tile(shape, F32, name="inv")
             ddep = work.tile(shape, F32, name="ddep")
-            taken = work.tile(shape, F32, name="taken")
-            grad = work.tile(shape, F32, name="grad")
+            minus_sq = work.tile(shape, F32, name="minus_sq")
+            terms = work.tile([P, 2, shape[1]], F32, name="terms")
             nc.scalar.activation(root[:], depth_sums[:, 1, :], ACT.Abs_reciprocal_sqrt, bias=0.5)
             nc.scalar.activation(inv[:], root[:], ACT.Square)
             nc.vector.tensor_tensor(ddep[:], depth_sums[:, 0, :], inv[:], ALU.mult)
-            nc.vector.tensor_tensor(taken[:], pose_sums[:, 1, :], ddep[:], ALU.mult)
-            nc.vector.tensor_tensor(grad[:], pose_sums[:, 0, :], taken[:], ALU.subtract)
-            nc.vector.tensor_tensor(both, grad[:], ddep[:], ALU.mult)
+            nc.vector.scalar_tensor_tensor(minus_sq[:], ddep[:], -1.0, ddep[:], ALU.mult, ALU.mult)
+            nc.vector.tensor_tensor(terms[:, 0, :], pose_sums[:, 0, :], ddep[:], ALU.mult)
+            nc.vector.tensor_tensor(terms[:, 1, :], pose_sums[:, 1, :], minus_sq[:], ALU.mult)
+            return terms
 
-        def make_table(t, both):
-            back = psum.tile([P, V], F32, name="back", bufs=1)
-            for h in range(HALVES):
-                nc.tensor.transpose(back[:, h * PTS : (h + 1) * PTS], both[:, h * P : (h + 1) * P], ident[:])
-            table = work.tile([P, V], F32, name="table")
-            nc.scalar.activation(table[:], back[:], ACT.Copy, scale=unit_sb[:, t : t + 1])
-            return table
+        def fill_table(t, table_cols, terms):
+            width = terms.shape[2]
+            back = psum.tile([P, width], F32, name="back", bufs=1)
+            for c in range(0, width, P):
+                point_sums(back[:, c : c + P], terms[:, :, c : c + P])
+            nc.scalar.activation(table_cols, back[:], ACT.Copy, scale=unit_sb[:, t : t + 1])
 
         def look_up(t, table, on_vector):
             cols = SLOT_GATHER // LIST_ROWS
@@ -219,15 +223,13 @@ def tile_picked_yschur_mul_p_kernel(
 
         units = [(t, h) for t in range(PACK) for h in range(HALVES)]
         last = PACK - 1
-        sums, both, tables = {}, {}, {}
+        sums, terms, tables = {}, {}, {}
         ready = prepare(*units[0])
         for u, (t, h) in enumerate(units):
             current = ready
             if u + 1 < len(units):
                 ready = prepare(*units[u + 1])
             depth, pose = multiply(*current)
-            if h == 0:
-                both[t] = work.tile([P, HALVES * P], F32, name="both")
             if t < last:
                 if h == 0:
                     sums[t] = sum_banks(HALVES * P)
@@ -237,21 +239,27 @@ def tile_picked_yschur_mul_p_kernel(
                 sums[t, h] = sum_banks(P)
                 add_up(depth, pose, sums[t, h][0][:], sums[t, h][1][:], h == 0)
             if t > 0 and h == 0:
-                eliminate(sums[t - 1][0][:], sums[t - 1][1][:], both[t - 1][:])
+                terms[t - 1] = eliminate(sums[t - 1][0][:], sums[t - 1][1][:])
                 if t > 1:
                     look_up(t - 2, tables[t - 2], 0)
             if t > 0 and h == 1:
-                tables[t - 1] = make_table(t - 1, both[t - 1])
+                tables[t - 1] = work.tile([P, V], F32, name="table")
+                fill_table(t - 1, tables[t - 1][:], terms[t - 1])
+        tables[last] = work.tile([P, V], F32, name="table")
         for h in range(HALVES):
-            eliminate(sums[last, h][0][:], sums[last, h][1][:], both[last][:, h * P : (h + 1) * P])
-        look_up(last - 1, tables[last - 1], 0)
-        look_up(last, make_table(last, both[last]), 2)
+            half_terms = eliminate(sums[last, h][0][:], sums[last, h][1][:])
+            fill_table(last, tables[last][:, h * PTS : (h + 1) * PTS], half_terms)
+        look_up(last - 1, tables[last - 1], 2)
+        look_up(last, tables[last], 2)
 
         out_rows = out.rearrange("(m p) r -> p m r", p=P)
         for s in range(U // SLOT_HALF):
             slots = slice(s * SLOT_HALF, (s + 1) * SLOT_HALF)
             hid = work.tile([P, SLOT_HALF, PACK], BF16, name="hid", align_bytes=64)
-            nc.vector.tensor_copy(hid[:], planes[:, :, slots].rearrange("p t r -> p r t"))
+            if s == 0:
+                nc.vector.tensor_copy(hid[:], planes[:, :, slots].rearrange("p t r -> p r t"))
+            else:
+                nc.scalar.copy(hid[:], planes[:, :, slots].rearrange("p t r -> p r t"))
             hw = work.tile([P, SLOT_HALF], U32, name="hw", align_bytes=64)
             hs = work.tile([P, SLOT_HALF], U8, name="hs", align_bytes=64)
             nc.vector.quantize_mx(hw[:].bitcast(FP8X4), hs[:], hid[:].rearrange("p r t -> p (r t)"))
@@ -271,4 +279,8 @@ def tile_picked_yschur_mul_p_kernel(
                     nc.scalar.copy(staged[:, m, :], acc[:, :SLOT_HALF])
                 else:
                     nc.vector.tensor_copy(staged[:, m, :], acc[:, :SLOT_HALF])
-            nc.sync.dma_start(out_rows[:, :, slots], staged[:])
+            if s == 0:
+                nc.sync.dma_start(out_rows[:, :, slots], staged[:])
+            else:
+                nc.scalar.dma_start(out_rows[:, 0, slots], staged[:, 0, :])
+                nc.sync.dma_start(out_rows[:, 1, slots], staged[:, 1, :])

@@ -144,66 +144,74 @@ def tile_picked_yschur_mul_p_kernel(
                     stop=(o == PASSES - 1),
                 )
 
-        def point_sums(sums, terms):
-            count = terms.shape[1]
-            for d in range(count):
+        def point_sums(sums, blocks):
+            for n, block in enumerate(blocks):
                 nc.tensor.matmul(
-                    sums, lhsT=terms[:, d, :], rhs=ident[:], is_transpose=True, start=(d == 0), stop=(d == count - 1)
+                    sums, lhsT=block, rhs=ident[:], is_transpose=True, start=(n == 0), stop=(n == len(blocks) - 1)
                 )
 
         def by_member(cols):
             return cols.rearrange("p (v d) -> p d v", d=D)
 
-        def prepare(t, h):
-            res_dv = work.tile([P, D, PTS], F32, name="res_dv", bufs=3)
-            nc.gpsimd.tensor_copy(res_dv[:], by_member(res_sb[:, t, BANK * h : BANK * (h + 1)]))
+        def by_pair(cols):
+            return cols.rearrange("p (v u e) -> p v u e", u=2, e=2)
+
+        def products(t, h):
             jd = psum.tile([P, BANK], F32, name="jd", tag="product", bufs=3)
             product(jd, 0, t, h)
             jp = psum.tile([P, BANK], F32, name="jp", tag="product", bufs=3)
             product(jp, 1, t, h)
-            return res_dv, jd, jp
+            return jd, jp
 
-        def multiply(res_dv, jd, jp):
-            depth = work.tile([P, 2, D, PTS], F32, name="depth")
+        def multiply(t, h, jd, jp):
+            res_cols = by_pair(res_sb[:, t, BANK * h : BANK * (h + 1)])
+            depth = work.tile([P, 2, BANK], F32, name="depth")
             jd_sb = work.tile([P, D, PTS], F32, name="jd_sb")
-            pose = work.tile([P, 2, D, PTS], F32, name="pose")
+            pose = work.tile([P, 2, BANK], F32, name="pose")
             nc.scalar.copy(jd_sb[:], by_member(jd[:]))
-            nc.vector.tensor_tensor(depth[:, 0, :, :], by_member(jd[:]), res_dv[:], ALU.mult)
-            nc.scalar.activation(depth[:, 1, :, :], jd_sb[:], ACT.Square)
-            nc.vector.tensor_tensor(pose[:, 0, :, :], by_member(jp[:]), res_dv[:], ALU.mult)
-            nc.vector.tensor_tensor(pose[:, 1, :, :], by_member(jp[:]), jd_sb[:], ALU.mult)
+            nc.vector.tensor_tensor(
+                depth[:, 0, :].rearrange("p (u v e) -> p v u e", u=2, e=2), by_pair(jd[:]), res_cols, ALU.mult
+            )
+            nc.scalar.activation(depth[:, 1, :], jd_sb[:].rearrange("p d v -> p (d v)"), ACT.Square)
+            nc.vector.tensor_tensor(
+                pose[:, 0, :].rearrange("p (u v e) -> p v u e", u=2, e=2), by_pair(jp[:]), res_cols, ALU.mult
+            )
+            nc.vector.tensor_tensor(
+                pose[:, 1, :].rearrange("p (d v) -> p d v", d=D), by_member(jp[:]), jd_sb[:], ALU.mult
+            )
             return depth, pose
 
-        def add_up(depth, pose, depth_sums, pose_sums, fold):
+        def add_up(terms, sums, fold):
             if fold:
-                folded = work.tile([P, 2, D // 2, PTS], F32, name="folded")
-                nc.gpsimd.tensor_tensor(folded[:], depth[:, :, : D // 2, :], depth[:, :, D // 2 :, :], ALU.add)
-                depth = folded
-            order = ((pose, pose_sums), (depth, depth_sums)) if fold else ((depth, depth_sums), (pose, pose_sums))
-            for terms, sums in order:
-                for i in range(2):
-                    point_sums(sums[:, i, :], terms[:, i, :, :])
+                folded = work.tile([P, 2, BANK // 2], F32, name="folded", bufs=3)
+                nc.gpsimd.tensor_tensor(folded[:], terms[:, :, : BANK // 2], terms[:, :, BANK // 2 :], ALU.add)
+                terms = folded
+            width = terms.shape[2]
+            pair_runs = range(0, width, 2 * PTS)
+            point_sums(sums[:, 0, :], [terms[:, 0, c + e : c + 2 * PTS : 2] for c in pair_runs for e in range(2)])
+            point_sums(sums[:, 1, :], [terms[:, 1, c : c + PTS] for c in range(0, width, PTS)])
 
         def eliminate(depth_sums, pose_sums):
             shape = [P, depth_sums.shape[2]]
             root = work.tile(shape, F32, name="root")
             inv = work.tile(shape, F32, name="inv")
             ddep = work.tile(shape, F32, name="ddep")
-            minus_sq = work.tile(shape, F32, name="minus_sq")
-            terms = work.tile([P, 2, shape[1]], F32, name="terms")
+            taken = work.tile(shape, F32, name="taken")
+            grad = work.tile(shape, F32, name="grad")
+            both = work.tile(shape, F32, name="both")
             nc.scalar.activation(root[:], depth_sums[:, 1, :], ACT.Abs_reciprocal_sqrt, bias=0.5)
             nc.scalar.activation(inv[:], root[:], ACT.Square)
             nc.vector.tensor_tensor(ddep[:], depth_sums[:, 0, :], inv[:], ALU.mult)
-            nc.vector.scalar_tensor_tensor(minus_sq[:], ddep[:], -1.0, ddep[:], ALU.mult, ALU.mult)
-            nc.vector.tensor_tensor(terms[:, 0, :], pose_sums[:, 0, :], ddep[:], ALU.mult)
-            nc.vector.tensor_tensor(terms[:, 1, :], pose_sums[:, 1, :], minus_sq[:], ALU.mult)
-            return terms
+            nc.vector.tensor_tensor(taken[:], pose_sums[:, 1, :], ddep[:], ALU.mult)
+            nc.vector.tensor_tensor(grad[:], pose_sums[:, 0, :], taken[:], ALU.subtract)
+            nc.vector.tensor_tensor(both[:], grad[:], ddep[:], ALU.mult)
+            return both
 
-        def fill_table(t, table_cols, terms):
-            width = terms.shape[2]
+        def fill_table(t, table_cols, both):
+            width = both.shape[1]
             back = psum.tile([P, width], F32, name="back", bufs=1)
             for c in range(0, width, P):
-                point_sums(back[:, c : c + P], terms[:, :, c : c + P])
+                nc.tensor.transpose(back[:, c : c + P], both[:, c : c + P], ident[:])
             nc.scalar.activation(table_cols, back[:], ACT.Copy, scale=unit_sb[:, t : t + 1])
 
         def look_up(t, table, on_vector):
@@ -224,20 +232,22 @@ def tile_picked_yschur_mul_p_kernel(
         units = [(t, h) for t in range(PACK) for h in range(HALVES)]
         last = PACK - 1
         sums, terms, tables = {}, {}, {}
-        ready = prepare(*units[0])
+        ready = products(*units[0])
         for u, (t, h) in enumerate(units):
             current = ready
             if u + 1 < len(units):
-                ready = prepare(*units[u + 1])
-            depth, pose = multiply(*current)
+                ready = products(*units[u + 1])
+            depth, pose = multiply(t, h, *current)
             if t < last:
                 if h == 0:
                     sums[t] = sum_banks(HALVES * P)
                 cols = slice(h * P, (h + 1) * P)
-                add_up(depth, pose, sums[t][0][:, :, cols], sums[t][1][:, :, cols], True)
+                add_up(depth, sums[t][0][:, :, cols], True)
+                add_up(pose, sums[t][1][:, :, cols], True)
             else:
                 sums[t, h] = sum_banks(P)
-                add_up(depth, pose, sums[t, h][0][:], sums[t, h][1][:], h == 0)
+                add_up(depth, sums[t, h][0][:], h == 0)
+                add_up(pose, sums[t, h][1][:], h == 0)
             if t > 0 and h == 0:
                 terms[t - 1] = eliminate(sums[t - 1][0][:], sums[t - 1][1][:])
                 if t > 1:

from contextlib import ExitStack

import concourse.mybir as mybir
from concourse.masks import make_identity

K, T, S, D, N, H, V, U = 1024, 4096, 1024, 4, 256, 512, 256, 512
FLOPS = 2 * (2 * K * H * S + H * N * U)

F32 = mybir.dt.float32
BF16 = mybir.dt.bfloat16
I32 = mybir.dt.int32
U32 = mybir.dt.uint32
U16 = mybir.dt.uint16
U8 = mybir.dt.uint8
FP8X4 = mybir.dt.float8_e4m3fn_x4
FP4X4 = mybir.dt.float4_e2m1fn_x4
ACT = mybir.ActivationFunctionType
ALU = mybir.AluOpType

P = 128
PACK = 4
PASSES = K // (P * PACK)
BANK = 512
HALVES = S // BANK
PTS = BANK // D
LIST_ROWS = 16
SLOT_GATHER = 128
SLOT_HALF = 256
SCALE_ROWS = 16
COPIES = P // (PASSES * SCALE_ROWS)
PLANE = S + 2 * H
TABLE_BYTES = 4 * T
X_SCALES_AT = 2 * TABLE_BYTES


def tile_picked_yschur_mul_p_kernel(
    tc, x_words, x_scales, w1_words, w1_scales, w2_words, w2_scales, res, unit, w3_words, w3_scales, offs, lmk, out
):
    nc = tc.nc
    with ExitStack() as ctx:
        keep = ctx.enter_context(tc.tile_pool(name="keep", bufs=1))
        work = ctx.enter_context(tc.tile_pool(name="work", bufs=2))
        shared = ctx.enter_context(tc.tile_pool(name="shared", bufs=1))
        psum = ctx.enter_context(tc.psum_pool(name="psum", bufs=1))

        offs_sb = keep.tile([P, S // LIST_ROWS], U16, name="offs_sb")
        lmk_sb = keep.tile([P, U // LIST_ROWS], U16, name="lmk_sb")
        unit_sb = keep.tile([P, PACK], F32, name="unit_sb")
        nc.sync.dma_start(offs_sb[:], offs)
        nc.sync.dma_start(lmk_sb[:], lmk)
        nc.sync.dma_start(unit_sb[:], unit.rearrange("(p t) o -> p (t o)", t=PACK))

        def load_scale_rows(dst, scales):
            rows = scales.rearrange("o r c -> (o r) c").bitcast(I32)
            nc.sync.dma_start(dst.bitcast(I32), rows.unsqueeze(1).to_broadcast([rows.shape[0], COPIES, rows.shape[1]]))

        xs_table = shared.tile([P, T], U8, name="xs_table", align_bytes=64, offset=X_SCALES_AT)
        load_scale_rows(xs_table[:], x_scales)
        ws_raw = keep.tile([P, 2, H], U8, name="ws_raw", align_bytes=64)
        for i, w_scales in enumerate((w1_scales, w2_scales)):
            load_scale_rows(ws_raw[:, i, :], w_scales)
        ww_raw = [keep.tile([P, PASSES, 2 * H], U8, name=f"ww_raw{i}", align_bytes=64) for i in range(2)]
        for i, w_words in enumerate((w1_words, w2_words)):
            nc.sync.dma_start(ww_raw[i][:].bitcast(I32), w_words.rearrange("o p c -> p o c").bitcast(I32))
        xw_table = []

        def load_table(o):
            xw_table.append(shared.tile([P, T], U32, name=f"xw_table{o}", align_bytes=64, offset=o * TABLE_BYTES))
            nc.sync.dma_start(xw_table[o][:].bitcast(I32), x_words[o].rearrange("p n t -> p (n t)").bitcast(I32))

        load_table(0)

        plane = [keep.tile([P, PLANE], U8, name=f"plane{o}", align_bytes=64) for o in range(PASSES)]
        for o in range(PASSES):
            nc.vector.memset(plane[o][:].bitcast(I32), 0)
        ident = keep.tile([P, P], F32, name="ident")
        make_identity(nc, ident[:])

        xs_picked = shared.tile([P, S], U8, name="xs_picked", align_bytes=64, offset=TABLE_BYTES)
        scale_rows = keep.tile([P, PLANE], U8, name="scale_rows", align_bytes=64)
        nc.vector.tensor_copy(xs_picked[:], xs_table[:].indirect(offs_sb[:]))
        nc.vector.tensor_copy(
            scale_rows[:, S:].rearrange("p (i t m) -> p i t m", i=2, t=PACK),
            ws_raw[:].rearrange("p i (m t) -> p i t m", t=PACK),
        )
        nc.vector.tensor_copy(scale_rows[:, :S].bitcast(I32), xs_picked[:].bitcast(I32))

        def place_scales(o):
            for q in range(4):
                first = COPIES * (SCALE_ROWS * o + 4 * q)
                nc.sync.dma_start(
                    plane[o][32 * q : 32 * q + 4, :].bitcast(I32),
                    scale_rows[first : first + 4 * COPIES : COPIES, :].bitcast(I32),
                )

        place_scales(0)
        load_table(1)
        place_scales(1)

        ww = []
        for i in range(2):
            ww.append(
                shared.tile(
                    [P, PASSES, 2 * H], U8, name=f"ww{i}", align_bytes=64, offset=X_SCALES_AT + i * PASSES * 2 * H
                )
            )
            nc.vector.tensor_copy(
                ww[i][:].rearrange("p o (t m b) -> p o t m b", t=PACK, b=2),
                ww_raw[i][:].rearrange("p o (m t b) -> p o t m b", t=PACK, b=2),
            )

        xw = [[keep.tile([P, BANK], U32, name=f"xw{o}_{h}", align_bytes=64) for h in range(HALVES)] for o in range(PASSES)]

        def gather_words(o):
            cols = BANK // LIST_ROWS
            for h in range(HALVES):
                nc.vector.tensor_copy(xw[o][h][:], xw_table[o][:].indirect(offs_sb[:, h * cols : (h + 1) * cols]))

        gather_words(0)
        res_rows = res.rearrange("(p t) s -> p t s", t=PACK)
        res_sb = shared.tile([P, PACK, S], F32, name="res_sb", align_bytes=64, offset=0)
        for t in range(PACK):
            nc.sync.dma_start(res_sb[:, t, :], res_rows[:, t, :])
        gather_words(1)

        w3w = shared.tile([P, 2 * N], U8, name="w3w", align_bytes=64, offset=TABLE_BYTES)
        nc.sync.dma_start(w3w[:].bitcast(I32), w3_words[0].bitcast(I32))
        w3s = shared.tile([P, N], U8, name="w3s", align_bytes=64, offset=TABLE_BYTES + 2 * N)
        nc.gpsimd.memset(w3s[:].bitcast(I32), 0)
        for q in range(4):
            nc.sync.dma_start(w3s[32 * q : 32 * q + 4, :].bitcast(I32), w3_scales[0, 4 * q : 4 * q + 4, :].bitcast(I32))

        planes = keep.tile([P, PACK, U], BF16, name="planes", align_bytes=64)

        def product(acc, i, t, h):
            for o in range(PASSES):
                nc.tensor.matmul_mx(
                    acc[:],
                    lhsT=ww[i][:, o, 2 * P * t : 2 * P * (t + 1)].bitcast(FP4X4),
                    lhsT_scale=plane[o][:, S + H * i + P * t : S + H * i + P * (t + 1)],
                    rhs=xw[o][h][:].bitcast(FP8X4),
                    rhs_scale=plane[o][:, BANK * h : BANK * (h + 1)],
                    start=(o == 0),
                    stop=(o == PASSES - 1),
                )

        def point_sums(sums, blocks):
            for n, block in enumerate(blocks):
                nc.tensor.matmul(
                    sums, lhsT=block, rhs=ident[:], is_transpose=True, start=(n == 0), stop=(n == len(blocks) - 1)
                )

        def by_member(cols):
            return cols.rearrange("p (v d) -> p d v", d=D)

        def by_pair(cols):
            return cols.rearrange("p (v u e) -> p v u e", u=2, e=2)

        def products(t, h):
            jd = psum.tile([P, BANK], F32, name="jd", tag="product", bufs=3)
            product(jd, 0, t, h)
            jp = psum.tile([P, BANK], F32, name="jp", tag="product", bufs=3)
            product(jp, 1, t, h)
            return jd, jp

        def multiply(t, h, jd, jp):
            res_cols = by_pair(res_sb[:, t, BANK * h : BANK * (h + 1)])
            depth = work.tile([P, 2, BANK], F32, name="depth")
            jd_sb = work.tile([P, D, PTS], F32, name="jd_sb")
            pose = work.tile([P, 2, BANK], F32, name="pose")
            nc.scalar.copy(jd_sb[:], by_member(jd[:]))
            nc.vector.tensor_tensor(
                depth[:, 0, :].rearrange("p (u v e) -> p v u e", u=2, e=2), by_pair(jd[:]), res_cols, ALU.mult
            )
            nc.scalar.activation(depth[:, 1, :], jd_sb[:].rearrange("p d v -> p (d v)"), ACT.Square)
            nc.vector.tensor_tensor(
                pose[:, 0, :].rearrange("p (u v e) -> p v u e", u=2, e=2), by_pair(jp[:]), res_cols, ALU.mult
            )
            nc.vector.tensor_tensor(
                pose[:, 1, :].rearrange("p (d v) -> p d v", d=D), by_member(jp[:]), jd_sb[:], ALU.mult
            )
            return depth, pose

        def add_up(terms, sums, fold):
            if fold:
                folded = work.tile([P, 2, BANK // 2], F32, name="folded", bufs=3)
                nc.gpsimd.tensor_tensor(folded[:], terms[:, :, : BANK // 2], terms[:, :, BANK // 2 :], ALU.add)
                terms = folded
            width = terms.shape[2]
            pair_runs = range(0, width, 2 * PTS)
            point_sums(sums[:, 0, :], [terms[:, 0, c + e : c + 2 * PTS : 2] for c in pair_runs for e in range(2)])
            point_sums(sums[:, 1, :], [terms[:, 1, c : c + PTS] for c in range(0, width, PTS)])

        def eliminate(depth_sums, pose_sums):
            shape = [P, depth_sums.shape[2]]
            root = work.tile(shape, F32, name="root")
            inv = work.tile(shape, F32, name="inv")
            ddep = work.tile(shape, F32, name="ddep")
            taken = work.tile(shape, F32, name="taken")
            grad = work.tile(shape, F32, name="grad")
            both = work.tile(shape, F32, name="both")
            nc.scalar.activation(root[:], depth_sums[:, 1, :], ACT.Abs_reciprocal_sqrt, bias=0.5)
            nc.scalar.activation(inv[:], root[:], ACT.Square)
            nc.vector.tensor_tensor(ddep[:], depth_sums[:, 0, :], inv[:], ALU.mult)
            nc.vector.tensor_tensor(taken[:], pose_sums[:, 1, :], ddep[:], ALU.mult)
            nc.vector.tensor_tensor(grad[:], pose_sums[:, 0, :], taken[:], ALU.subtract)
            nc.vector.tensor_tensor(both[:], grad[:], ddep[:], ALU.mult)
            return both

        def fill_table(t, table_cols, both):
            width = both.shape[1]
            back = psum.tile([P, width], F32, name="back", bufs=1)
            for c in range(0, width, P):
                nc.tensor.transpose(back[:, c : c + P], both[:, c : c + P], ident[:])
            nc.scalar.activation(table_cols, back[:], ACT.Copy, scale=unit_sb[:, t : t + 1])

        def look_up(t, table, on_vector):
            cols = SLOT_GATHER // LIST_ROWS
            for c in range(U // SLOT_GATHER):
                picked = table[:].indirect(lmk_sb[:, c * cols : (c + 1) * cols])
                dst = planes[:, t, c * SLOT_GATHER : (c + 1) * SLOT_GATHER]
                if c < on_vector:
                    nc.vector.tensor_copy(dst, picked)
                else:
                    nc.scalar.activation(dst, picked, ACT.Copy)

        def sum_banks(width):
            depth_sums = psum.tile([P, 2, width], F32, name="depth_sums", bufs=2)
            pose_sums = psum.tile([P, 2, width], F32, name="pose_sums", bufs=2)
            return depth_sums, pose_sums

        units = [(t, h) for t in range(PACK) for h in range(HALVES)]
        last = PACK - 1
        sums, terms, tables = {}, {}, {}
        ready = products(*units[0])
        for u, (t, h) in enumerate(units):
            current = ready
            if u + 1 < len(units):
                ready = products(*units[u + 1])
            depth, pose = multiply(t, h, *current)
            if t < last:
                if h == 0:
                    sums[t] = sum_banks(HALVES * P)
                cols = slice(h * P, (h + 1) * P)
                add_up(depth, sums[t][0][:, :, cols], True)
                add_up(pose, sums[t][1][:, :, cols], True)
            else:
                sums[t, h] = sum_banks(P)
                add_up(depth, sums[t, h][0][:], h == 0)
                add_up(pose, sums[t, h][1][:], h == 0)
            if t > 0 and h == 0:
                terms[t - 1] = eliminate(sums[t - 1][0][:], sums[t - 1][1][:])
                if t > 1:
                    look_up(t - 2, tables[t - 2], 0)
            if t > 0 and h == 1:
                tables[t - 1] = work.tile([P, V], F32, name="table")
                fill_table(t - 1, tables[t - 1][:], terms[t - 1])
        tables[last] = work.tile([P, V], F32, name="table")
        for h in range(HALVES):
            half_terms = eliminate(sums[last, h][0][:], sums[last, h][1][:])
            fill_table(last, tables[last][:, h * PTS : (h + 1) * PTS], half_terms)
        look_up(last - 1, tables[last - 1], 2)
        look_up(last, tables[last], 2)

        out_rows = out.rearrange("(m p) r -> p m r", p=P)
        for s in range(U // SLOT_HALF):
            slots = slice(s * SLOT_HALF, (s + 1) * SLOT_HALF)
            hid = work.tile([P, SLOT_HALF, PACK], BF16, name="hid", align_bytes=64)
            if s == 0:
                nc.vector.tensor_copy(hid[:], planes[:, :, slots].rearrange("p t r -> p r t"))
            else:
                nc.scalar.copy(hid[:], planes[:, :, slots].rearrange("p t r -> p r t"))
            hw = work.tile([P, SLOT_HALF], U32, name="hw", align_bytes=64)
            hs = work.tile([P, SLOT_HALF], U8, name="hs", align_bytes=64)
            nc.vector.quantize_mx(hw[:].bitcast(FP8X4), hs[:], hid[:].rearrange("p r t -> p (r t)"))
            staged = work.tile([P, N // P, SLOT_HALF], F32, name="staged")
            for m in range(N // P):
                acc = psum.tile([P, BANK], F32, name="acc", tag="product", bufs=3)
                nc.tensor.matmul_mx(
                    acc[:, :SLOT_HALF],
                    lhsT=w3w[:, 2 * P * m : 2 * P * (m + 1)].bitcast(FP4X4),
                    lhsT_scale=w3s[:, P * m : P * (m + 1)],
                    rhs=hw[:].bitcast(FP8X4),
                    rhs_scale=hs[:],
                    start=True,
                    stop=True,
                )
                if m == 0:
                    nc.scalar.copy(staged[:, m, :], acc[:, :SLOT_HALF])
                else:
                    nc.vector.tensor_copy(staged[:, m, :], acc[:, :SLOT_HALF])
            if s == 0:
                nc.sync.dma_start(out_rows[:, :, slots], staged[:])
            else:
                nc.scalar.dma_start(out_rows[:, 0, slots], staged[:, 0, :])
                nc.sync.dma_start(out_rows[:, 1, slots], staged[:, 1, :])
